import numpy as np
import ml_dtypes


def mxq(x, axis, fmt="e4m3"):
    dtype, down = {"e4m3": (ml_dtypes.float8_e4m3fn, 7), "e5m2": (ml_dtypes.float8_e5m2, 14)}[fmt]
    v = np.moveaxis(np.asarray(x, np.float32).astype(ml_dtypes.bfloat16).astype(np.float64), axis, -1)
    blocks = v.reshape(v.shape[:-1] + (-1, 32))
    amax = np.abs(blocks).max(-1, keepdims=True)
    byte = np.maximum(np.where(amax > 0, np.frexp(amax)[1] - 1 + 127, 0) - down, 1)
    scale = np.exp2(byte - 127.0)
    codes = (blocks / scale).astype(np.float32).astype(dtype).astype(np.float64)
    return np.moveaxis((codes * scale).reshape(v.shape), -1, axis)


WIDE = False


def mx_kscale(k):
    if not WIDE:
        return np.ones(k)
    levels = np.array([10, -10, 5, -5, 0])
    if k % 512:
        return np.exp2(np.random.permutation(np.resize(levels, k // 32))).repeat(32)
    a = np.empty((k // 512, 16))
    for p in range(k // 512):
        a[p, :8] = np.random.permutation(np.resize(levels, 8))
        for g in range(8):
            far = levels[np.abs(levels - a[p, g]) >= 10]
            a[p, g + 8] = far[np.random.randint(len(far))]
    return np.exp2(a.ravel()).repeat(32)


def f64(x):
    return np.asarray(x).astype(np.float64)


def striped(idx):
    return np.tile(idx.reshape(-1, 16).T, (8, 1)).astype(np.uint16)


def unstriped(offs):
    return offs[:16].T.reshape(-1).astype(np.int64)


E2M1 = np.array([0.0, 0.5, 1.0, 1.5, 2.0, 3.0, 4.0, 6.0, -0.0, -0.5, -1.0, -1.5, -2.0, -3.0, -4.0, -6.0])


def pack_weight(w, fmt):
    k, n = w.shape
    w = f64(np.asarray(w, np.float32).astype(ml_dtypes.bfloat16)).reshape(k // 32, 32, n)
    amax = np.abs(w).max(1)
    if fmt == "e4m3":
        byte = np.frexp(amax)[1] - 1 + 127 - 7
    else:
        mant, ex = np.frexp(amax / 6.0)
        byte = np.where(mant > 0.5, ex, ex - 1) + 127
    byte = np.clip(np.where(amax > 0, byte, 1), 1, 254)
    scaled = (w * np.exp2(127.0 - byte)[:, None, :]).reshape(k, n).astype(np.float32)
    by_word = np.ascontiguousarray(scaled.reshape(k // 512, 128, 4, n).transpose(0, 1, 3, 2))
    if fmt == "e4m3":
        words = by_word.astype(ml_dtypes.float8_e4m3fn).view(np.uint8)
    else:
        c = by_word.astype(ml_dtypes.float4_e2m1fn).view(np.uint8) & 0xF
        words = (c[..., 0::2] | (c[..., 1::2] << 4)).reshape(k // 512, 128, 2 * n)
    return np.ascontiguousarray(words), np.ascontiguousarray(byte.astype(np.uint8).reshape(k // 512, 16, n))


def unpack_weight(words, scales, fmt):
    g, _, n = scales.shape
    words = np.ascontiguousarray(words).reshape(g, 128, n, -1)
    if fmt == "e4m3":
        vals = words.view(ml_dtypes.float8_e4m3fn).astype(np.float64)
    else:
        nib = np.empty((g, 128, n, 4), np.uint8)
        nib[..., 0::2] = words & 0xF
        nib[..., 1::2] = words >> 4
        vals = E2M1[nib]
    vals = vals * np.repeat(np.exp2(scales.astype(np.float64) - 127.0), 8, axis=1)[..., None]
    return vals.transpose(0, 1, 3, 2).reshape(g * 512, n)


def gelu(v):
    return 0.5 * v * (1.0 + np.tanh(np.sqrt(2.0 / np.pi) * (v + 0.044715 * v**3)))


K, R, H, T, S, S2, T3, T2, P = 1024, 512, 1024, 2048, 512, 512, 1024, 1024, 512

def setup_inputs():
    n = np.random.standard_normal
    s, ur, u = mx_kscale(K)[:, None], mx_kscale(R)[:, None], mx_kscale(H)[:, None]
    tab_words, tab_scales = pack_weight(n((K, T)) * s, "e4m3")
    tab2_words, tab2_scales = pack_weight(n((H, T3)) / np.sqrt(H) / u, "e4m3")
    w4_words, w4_scales = pack_weight(n((K, H)) / np.sqrt(K) / s, "e2m1")
    return {
        "tab_words": tab_words, "tab_scales": tab_scales,
        "tab2_words": tab2_words, "tab2_scales": tab2_scales,
        "w4_words": w4_words, "w4_scales": w4_scales,
        "w1": (1.6 * n((K, R)) / np.sqrt(K) / s).astype(np.float32),
        "gain": (np.exp(0.3 * n(R)) * ur[:, 0]).astype(np.float32),
        "w2": (1.3 * n((R, H)) / np.sqrt(R) / ur * u.T).astype(np.float32),
        "res": (0.8 * n((H, S)) * u).astype(np.float32),
        "wgs": np.exp(0.3 * n((128, S))).astype(np.float32),
        "page0": (n((H, T2)) * u).astype(np.float32),
        "cutoff": (0.8 * n(S2)).astype(np.float32),
        "offs": striped(np.random.permutation(T)[:S]),
        "offs2": striped(np.random.permutation(T3)[:S2]),
        "offs3": striped(np.random.permutation(T2)[:S]),
        "pos1": striped(np.random.permutation(T2)[:P]),
        "pos2": striped(np.random.permutation(T2)[:P]),
    }

def reference(tab_words, tab_scales, tab2_words, tab2_scales, w4_words, w4_scales, w1, gain, w2, res, wgs, page0, cutoff, offs, offs2, offs3, pos1, pos2):
    v = unpack_weight(tab_words, tab_scales, "e4m3")[:, unstriped(offs)]
    v2 = unpack_weight(tab2_words, tab2_scales, "e4m3")[:, unstriped(offs2)]
    w4 = unpack_weight(w4_words, w4_scales, "e2m1")
    x = f64(gain)[:, None] * np.tanh(mxq(f64(w1), 0, "e4m3").T @ v)
    b = mxq(f64(w2), 0, "e4m3").T @ mxq(x, 0, "e4m3")
    d = w4.T @ v
    h = b * d + f64(res)
    page = f64(page0).copy()
    page[:, unstriped(offs3)] = np.tile(f64(wgs), (H // 128, 1)) * h
    e = v2.T @ mxq(page, 0, "e4m3")
    later = np.maximum(e[:, unstriped(pos2)], f64(cutoff)[:, None])
    return e[:, unstriped(pos1)] - later

@@ -1,0 +1,316 @@
+from contextlib import ExitStack
+
+import concourse.mybir as mybir
+
+K, R, H, T, S, T3, T2 = 1024, 512, 1024, 2048, 512, 1024, 1024
+FLOPS = 2 * (K * R * S + R * H * S + K * H * S + H * S * T2)
+
+F32 = mybir.dt.float32
+BF16 = mybir.dt.bfloat16
+I32 = mybir.dt.int32
+U32 = mybir.dt.uint32
+U16 = mybir.dt.uint16
+U8 = mybir.dt.uint8
+FP8X4 = mybir.dt.float8_e4m3fn_x4
+FP4X4 = mybir.dt.float4_e2m1fn_x4
+ALU = mybir.AluOpType
+ACT = mybir.ActivationFunctionType
+
+P = 128
+PACK = 4
+PASS = P * PACK
+BANK = 512
+QUAD = 32
+LIVE = 4
+
+
+def tile_list_dredge_streak_scores_kernel(
+    tc, tab_words, tab_scales, tab2_words, tab2_scales, w4_words, w4_scales, w1, gain, w2, res, wgs, page0, cutoff,
+    offs, offs2, offs3, pos1, pos2, out,
+):
+    nc = tc.nc
+    with ExitStack() as ctx:
+        keep = ctx.enter_context(tc.tile_pool(name="keep", bufs=1))
+        psum = ctx.enter_context(tc.psum_pool(name="psum", bufs=1))
+
+        def sb(name, shape, dtype, tag=None, bufs=1):
+            return keep.tile(shape, dtype, name=name, tag=tag or name, bufs=bufs, align_bytes=64)
+
+        def bank(b, name, shape):
+            return psum.tile(shape, F32, name=name, tag="bank%d" % b)
+
+        def load_list(name, src):
+            t = keep.tile([P, S // 16], U16, name=name)
+            nc.sync.dma_start(t[:], src)
+            return t
+
+        tab_plane = sb("tab_plane", [P, T], U8)
+        w4_plane_raw = sb("w4_plane_raw", [P, 2, H], U8)
+        tab2_plane = sb("tab2_plane", [P, T3], U8)
+        nc.gpsimd.memset(tab_plane[:].bitcast(I32), 0)
+        nc.vector.memset(w4_plane_raw[:].bitcast(I32), 0)
+        nc.gpsimd.memset(tab2_plane[:].bitcast(I32), 0)
+
+        def load_packed_plane(plane, src):
+            for q in range(4):
+                nc.sync.dma_start(
+                    plane[QUAD * q : QUAD * q + 2 * LIVE, :].bitcast(I32), src[:, LIVE * q : LIVE * (q + 1), :].bitcast(I32)
+                )
+
+        def load_words(name, src, width):
+            t = sb(name, [P, width], I32)
+            nc.sync.dma_start(t[:], src.rearrange("p t i -> p (t i)").bitcast(I32))
+            return t
+
+        def load_w1(name, a, cols):
+            t = sb(name, [P, PACK, cols.stop - cols.start], F32)
+            nc.sync.dma_start(t[:], w1[PASS * a : PASS * (a + 1), cols].rearrange("(p j) c -> p j c", j=PACK))
+            return t
+
+        w4_raw = sb("w4_raw", [P, 2, 2 * H], U8)
+        nc.sync.dma_start(w4_raw[:].bitcast(I32), w4_words.rearrange("a p c -> p a c").bitcast(I32))
+        idx = load_list("idx", offs)
+        gain_sb = sb("gain_sb", [P, PACK], F32)
+        nc.sync.dma_start(gain_sb[:], gain.rearrange("(p t) -> p t", t=PACK))
+        idx3 = load_list("idx3", offs3)
+        w1_raw0 = load_w1("w1_raw0", 0, slice(0, R))
+        load_packed_plane(tab_plane, tab_scales)
+        tab_w = [load_words("tab_w0", tab_words[0], T)]
+        for q in range(4):
+            nc.sync.dma_start(
+                w4_plane_raw[QUAD * q : QUAD * q + LIVE, :, :].bitcast(I32),
+                w4_scales[:, LIVE * q : LIVE * (q + 1), :].rearrange("a r c -> r a c").bitcast(I32),
+            )
+        tab_w.append(load_words("tab_w1", tab_words[1], T))
+        w1_raw1 = [load_w1("w1_raw1%d" % h, 1, slice(256 * h, 256 * (h + 1))) for h in range(2)]
+
+        w2_rows = w2.rearrange("(p j) c -> p j c", j=PACK)
+        wgs_rows = wgs.rearrange("(p t) j -> p t j", t=PACK)
+        res_rows = res.rearrange("(a p t) j -> a t p j", p=P, t=PACK)
+        page_rows = page0.rearrange("(a p t) c -> a t p c", p=P, t=PACK)
+        w2_raw = [sb("w2_raw%d" % a, [P, PACK, PASS], F32) for a in range(2)]
+        res_sb = [sb("res%d" % i, [P, S], F32) for i in range(8)]
+        page = [sb("page%d" % i, [P, T2], F32) for i in range(8)]
+        wg_first = sb("wg_first", [P, 1, S], F32)
+        wg_rest = sb("wg_last", [P, PACK - 1, S], F32)
+
+        def load_w2(a):
+            nc.sync.dma_start(w2_raw[a][:], w2_rows[:, :, PASS * a : PASS * (a + 1)])
+
+        def load_slice(i):
+            a, t = divmod(i, PACK)
+            nc.sync.dma_start(res_sb[i][:], res_rows[a, t])
+            nc.sync.dma_start(page[i][:], page_rows[a, t])
+
+        load_w2(0)
+        for q in range(4):
+            nc.sync.dma_start(wg_first[QUAD * q : QUAD * (q + 1), :, :], wgs_rows[:, 0:1, :])
+        load_slice(0)
+        for q in range(4):
+            nc.sync.dma_start(wg_rest[QUAD * q : QUAD * (q + 1), :, :], wgs_rows[:, 1:PACK, :])
+        load_slice(1)
+        load_w2(1)
+        for i in range(2, 8):
+            load_slice(i)
+        idx2 = load_list("idx2", offs2)
+        p1 = load_list("p1", pos1)
+        p2 = load_list("p2", pos2)
+        tab2_w = [load_words("tab2_w%d" % a, tab2_words[a], T3) for a in range(2)]
+        load_packed_plane(tab2_plane, tab2_scales)
+        cut_sb = sb("cut_sb", [P, S // P], F32)
+        with nc.allow_non_contiguous_dma(reason="one value a partition"):
+            nc.sync.dma_start(cut_sb[:], cutoff.rearrange("(m p) -> p m", p=P))
+
+        w4_codes = sb("w4_codes", [P, 2, 2 * H], U8)
+        w4_plane = sb("w4_plane", [P, 2, H], U8)
+        nc.vector.tensor_copy(
+            w4_codes[:].bitcast(U16).rearrange("p k (a t m) -> p (k a) t m", a=2, t=PACK),
+            w4_raw[:].bitcast(U16).rearrange("p k (a m t) -> p (k a) t m", a=2, t=PACK),
+        )
+        nc.vector.tensor_copy(
+            w4_plane[:].rearrange("p k (a t m) -> p (k a) t m", a=2, t=PACK),
+            w4_plane_raw[:].rearrange("p k (a m t) -> p (k a) t m", a=2, t=PACK),
+        )
+
+        def round_weight(copy, rounded, raw, first, lo, hi):
+            copy(
+                rounded[:].rearrange("p (t m j) -> p m t j", t=PACK, j=PACK)[:, lo:hi],
+                raw[:].rearrange("p j (m t) -> p m t j", t=PACK)[:, lo - first : hi - first],
+            )
+
+        def rounded_tile(name, tag):
+            return sb(name, [P, PACK * PASS], BF16, tag=tag)
+
+        def quantise(name, rounded, tag=None):
+            codes = sb(name + "_codes", [P, PASS], U32, tag=tag)
+            plane = sb(name + "_plane", [P, PASS], U8)
+            nc.vector.quantize_mx(out=codes[:].bitcast(FP8X4), scales=plane[:], in_=rounded[:])
+            return codes, plane
+
+        v_plane = sb("v_plane", [P, S], U8)
+        v_plane_moved = sb("v_plane_moved", [P, S], U8)
+        v_codes = [sb("v_codes%d" % a, [P, S], U32) for a in range(2)]
+        nc.vector.tensor_copy(v_plane[:], tab_plane[:].indirect(idx[:]))
+        for q in range(4):
+            nc.gpsimd.dma_start(
+                v_plane_moved[QUAD * q : QUAD * q + LIVE, :].bitcast(I32),
+                v_plane[QUAD * q + LIVE : QUAD * q + 2 * LIVE, :].bitcast(I32),
+            )
+        for a in range(2):
+            nc.vector.tensor_copy(v_codes[a][:], tab_w[a][:].bitcast(U32).indirect(idx[:]))
+
+        w1_bf = [rounded_tile("w1_bf%d" % a, "bf%d" % a) for a in range(2)]
+        round_weight(nc.scalar.copy, w1_bf[0], w1_raw0, 0, 0, P)
+        round_weight(nc.scalar.copy, w1_bf[1], w1_raw1[0], 0, 0, 64)
+        round_weight(nc.scalar.copy, w1_bf[1], w1_raw1[1], 64, 64, 88)
+        round_weight(nc.vector.tensor_copy, w1_bf[1], w1_raw1[1], 64, 88, P)
+        w1_q = [quantise("w1_%d" % a, w1_bf[a]) for a in range(2)]
+
+        z = [bank(q, "z%d" % q, [P, PACK, P]) for q in range(4)]
+        for a in range(2):
+            codes, plane = w1_q[a]
+            for q in range(4):
+                for t in range(PACK):
+                    nc.tensor.matmul_mx(
+                        out=z[q][:, t, :],
+                        lhsT=codes[:, P * t : P * (t + 1)].bitcast(FP8X4), lhsT_scale=plane[:, P * t : P * (t + 1)],
+                        rhs=v_codes[a][:, P * q : P * (q + 1)].bitcast(FP8X4), rhs_scale=v_plane[LIVE * a : P, P * q : P * (q + 1)],
+                        start=(a == 0 and t == 0), stop=(a == 1 and t == PACK - 1),
+                    )
+        x_codes = sb("x_codes", [P, S], U32)
+        x_plane = sb("x_plane", [P, S], U8)
+        x_bf = [sb("x_bf%d" % h, [P, 2, P, PACK], BF16) for h in range(2)]
+        for q in range(4):
+            th = sb("th%d" % q, [P, P, PACK], F32)
+            nc.scalar.activation(th[:], z[q][:].rearrange("p t n -> p n t"), ACT.Tanh)
+            nc.vector.tensor_tensor(
+                x_bf[q // 2][:, q % 2, :, :], th[:], gain_sb[:].unsqueeze(1).to_broadcast([P, P, PACK]), ALU.mult
+            )
+        w2_bf = [rounded_tile("w2_bf%d" % a, "bf%d" % (2 + a)) for a in range(2)]
+        round_weight(nc.scalar.copy, w2_bf[0], w2_raw[0], 0, 0, 80)
+        round_weight(nc.vector.tensor_copy, w2_bf[0], w2_raw[0], 0, 80, P)
+        for h in range(2):
+            nc.vector.quantize_mx(
+                out=x_codes[:, 256 * h : 256 * (h + 1)].bitcast(FP8X4), scales=x_plane[:, 256 * h : 256 * (h + 1)],
+                in_=x_bf[h][:].rearrange("p q n t -> p (q n t)"),
+            )
+        w2_q = [quantise("w2_0", w2_bf[0])]
+
+        page_bf = [[sb("page_bf%d%d" % (a, h), [P, BANK, PACK], BF16, tag="bf%d" % (2 * a + h)) for h in range(2)] for a in range(1)]
+        page_q = []
+
+        def other_product(i):
+            a, t = divmod(i, PACK)
+            cols = slice(PASS * a + P * t, PASS * a + P * (t + 1))
+            d = bank(i % 4, "d%d" % i, [P, S])
+            for k in range(2):
+                nc.tensor.matmul_mx(
+                    out=d[:],
+                    lhsT=w4_codes[:, k, 2 * cols.start : 2 * cols.stop].bitcast(FP4X4), lhsT_scale=w4_plane[:, k, cols],
+                    rhs=v_codes[k][:].bitcast(FP8X4), rhs_scale=(v_plane, v_plane_moved)[k][:],
+                    start=(k == 0), stop=(k == 1),
+                )
+            d_sb = sb("d_sb%d" % i, [P, S], F32)
+            nc.scalar.copy(d_sb[:], d[:])
+            return d_sb
+
+        d_all = [other_product(i) for i in range(8)]
+        round_weight(nc.scalar.copy, w2_bf[1], w2_raw[1], 0, 0, P)
+
+        def product(i):
+            a, t = divmod(i, PACK)
+            d_sb = d_all[i]
+            b = bank(4 + i % 4, "b%d" % i, [P, S])
+            codes, plane = w2_q[a]
+            nc.tensor.matmul_mx(
+                out=b[:],
+                lhsT=codes[:, P * t : P * (t + 1)].bitcast(FP8X4), lhsT_scale=plane[:, P * t : P * (t + 1)],
+                rhs=x_codes[:].bitcast(FP8X4), rhs_scale=x_plane[:], start=True, stop=True,
+            )
+            bd = sb("bd%d" % i, [P, S], F32, tag="bd", bufs=2)
+            nc.vector.tensor_tensor(bd[:], b[:], d_sb[:], ALU.mult)
+            return bd
+
+        def add_res(i, bd):
+            h_sb = sb("h%d" % i, [P, S], F32, tag="h%d" % (i % 2))
+            nc.vector.tensor_tensor(h_sb[:], bd[:], res_sb[i][:], ALU.add)
+            return h_sb
+
+        def refresh(i, h_sb):
+            a, t = divmod(i, PACK)
+            wg = wg_first[:, 0, :] if t == 0 else wg_rest[:, t - 1, :]
+            nc.vector.tensor_tensor(page[i][:].indirect(idx3[:]), h_sb[:], wg, ALU.mult)
+            for h in range(2):
+                nc.scalar.copy(page_bf[a][h][:, :, t], page[i][:, BANK * h : BANK * (h + 1)])
+
+        def quantise_page(a, tags):
+            return [quantise("page_%d%d" % (a, h), page_bf[a][h][:].rearrange("p c t -> p (c t)"), tags[h]) for h in range(2)]
+
+        h_next = add_res(0, product(0))
+        for i in range(8):
+            h_now = h_next
+            if i == 1:
+                w2_q.append(quantise("w2_1", w2_bf[1]))
+                page_bf.append([sb("page_bf1%d" % h, [P, BANK, PACK], BF16, tag="bf%d" % (2 + h)) for h in range(2)])
+            if i < 7:
+                bd_next = product(i + 1)
+            refresh(i, h_now)
+            if i < 7:
+                h_next = add_res(i + 1, bd_next)
+            if i == 6:
+                page_q.append(quantise_page(0, ["res6", "res7"]))
+
+        v2_plane = sb("v2_plane", [P, S], U8, tag="h1")
+        v2_codes = [sb("v2_codes0", [P, S], U32, tag="wg_last"), sb("v2_codes1", [P, S], U32, tag="h0")]
+        nc.vector.tensor_copy(v2_plane[:], tab2_plane[:].indirect(idx2[:]))
+        for a in range(2):
+            nc.vector.tensor_copy(v2_codes[a][:], tab2_w[a][:].bitcast(U32).indirect(idx2[:]))
+        page_q.append(quantise_page(1, [None, None]))
+
+        e_tags = ["tab_w0", "tab_w1", "w1_raw0", "w1_raw10"]
+
+        e_banks = [[None, None] for m in range(4)]
+
+        def score_pass(m, h, a):
+            codes, plane = page_q[a][h]
+            nc.tensor.matmul_mx(
+                out=e_banks[m][h][:],
+                lhsT=v2_codes[a][:, P * m : P * (m + 1)].bitcast(FP8X4),
+                lhsT_scale=v2_plane[LIVE * a : P, P * m : P * (m + 1)],
+                rhs=codes[:].bitcast(FP8X4), rhs_scale=plane[:], start=(a == 0), stop=(a == 1),
+            )
+
+        e_all = []
+        for pair in range(2):
+            for m in (2 * pair, 2 * pair + 1):
+                for h in range(2):
+                    e_banks[m][h] = bank(2 * (m % 2) + h, "e%d%d" % (m, h), [P, BANK])
+                    score_pass(m, h, 0)
+            for m in (2 * pair, 2 * pair + 1):
+                e_sb = sb("e%d" % m, [P, T2], F32, tag=e_tags[m])
+                for h in range(2):
+                    score_pass(m, h, 1)
+                    nc.scalar.copy(e_sb[:, BANK * h : BANK * (h + 1)], e_banks[m][h][:])
+                e_all.append(e_sb)
+
+        def pick_second(m, e_sb):
+            second = sb("second%d" % m, [P, S], F32, tag="second", bufs=2)
+            nc.vector.tensor_copy(second[:], e_sb[:].indirect(p2[:]))
+            return second
+
+        def floor_second(m, second):
+            later = sb("later%d" % m, [P, S], F32, tag="later", bufs=2)
+            nc.vector.tensor_scalar_max(later[:], second[:], cut_sb[:, m : m + 1])
+            return later
+
+        def finish(m, e_sb, later):
+            result = sb("result%d" % m, [P, S], F32, tag="result", bufs=3)
+            nc.vector.tensor_tensor(result[:], e_sb[:].indirect(p1[:]), later[:], ALU.subtract)
+            nc.sync.dma_start(out[P * m : P * (m + 1), :], result[:])
+
+        later = floor_second(0, pick_second(0, e_all[0]))
+        for m in range(1, 4):
+            second = pick_second(m, e_all[m])
+            finish(m - 1, e_all[m - 1], later)
+            later = floor_second(m, second)
+        finish(3, e_all[3], later)

@@ -110,13 +110,15 @@ def tile_list_dredge_streak_scores_kernel(
             nc.sync.dma_start(wg_rest[QUAD * q : QUAD * (q + 1), :, :], wgs_rows[:, 1:PACK, :])
         load_slice(1)
         load_w2(1)
-        for i in range(2, 8):
+        for i in range(2, 4):
             load_slice(i)
         idx2 = load_list("idx2", offs2)
         p1 = load_list("p1", pos1)
         p2 = load_list("p2", pos2)
         tab2_w = [load_words("tab2_w%d" % a, tab2_words[a], T3) for a in range(2)]
         load_packed_plane(tab2_plane, tab2_scales)
+        for i in range(4, 8):
+            load_slice(i)
         cut_sb = sb("cut_sb", [P, S // P], F32)
         with nc.allow_non_contiguous_dma(reason="one value a partition"):
             nc.sync.dma_start(cut_sb[:], cutoff.rearrange("(m p) -> p m", p=P))
@@ -227,41 +229,47 @@ def tile_list_dredge_streak_scores_kernel(
                 lhsT=codes[:, P * t : P * (t + 1)].bitcast(FP8X4), lhsT_scale=plane[:, P * t : P * (t + 1)],
                 rhs=x_codes[:].bitcast(FP8X4), rhs_scale=x_plane[:], start=True, stop=True,
             )
-            bd = sb("bd%d" % i, [P, S], F32, tag="bd", bufs=2)
+            bd = sb("bd%d" % i, [P, S], F32, tag="bd", bufs=3)
             nc.vector.tensor_tensor(bd[:], b[:], d_sb[:], ALU.mult)
             return bd
 
-        def add_res(i, bd):
-            h_sb = sb("h%d" % i, [P, S], F32, tag="h%d" % (i % 2))
-            nc.vector.tensor_tensor(h_sb[:], bd[:], res_sb[i][:], ALU.add)
-            return h_sb
-
-        def refresh(i, h_sb):
-            a, t = divmod(i, PACK)
+        def weigh(i, bd):
+            t = i % PACK
             wg = wg_first[:, 0, :] if t == 0 else wg_rest[:, t - 1, :]
-            nc.vector.tensor_tensor(page[i][:].indirect(idx3[:]), h_sb[:], wg, ALU.mult)
+            h_sb = sb("h%d" % i, [P, S], F32, tag="h", bufs=2)
+            nc.gpsimd.tensor_tensor(h_sb[:], bd[:], res_sb[i][:], ALU.add)
+            placed = sb("placed%d" % i, [P, S], F32, tag="placed%d" % (i % 2))
+            nc.gpsimd.tensor_tensor(placed[:], h_sb[:], wg, ALU.mult)
+            return placed
+
+        def round_page(i):
+            a, t = divmod(i, PACK)
             for h in range(2):
                 nc.scalar.copy(page_bf[a][h][:, :, t], page[i][:, BANK * h : BANK * (h + 1)])
 
         def quantise_page(a, tags):
             return [quantise("page_%d%d" % (a, h), page_bf[a][h][:].rearrange("p c t -> p (c t)"), tags[h]) for h in range(2)]
 
-        h_next = add_res(0, product(0))
-        for i in range(8):
-            h_now = h_next
-            if i == 1:
+        bd = product(0)
+        placed = weigh(1, product(1))
+        h_first = sb("h0", [P, S], F32)
+        nc.vector.tensor_tensor(h_first[:], bd[:], res_sb[0][:], ALU.add)
+        nc.vector.tensor_tensor(page[0][:].indirect(idx3[:]), h_first[:], wg_first[:, 0, :], ALU.mult)
+        round_page(0)
+        for i in range(1, 8):
+            now = placed
+            if i == 2:
                 w2_q.append(quantise("w2_1", w2_bf[1]))
                 page_bf.append([sb("page_bf1%d" % h, [P, BANK, PACK], BF16, tag="bf%d" % (2 + h)) for h in range(2)])
             if i < 7:
-                bd_next = product(i + 1)
-            refresh(i, h_now)
-            if i < 7:
-                h_next = add_res(i + 1, bd_next)
+                placed = weigh(i + 1, product(i + 1))
+            nc.vector.tensor_copy(page[i][:].indirect(idx3[:]), now[:])
+            round_page(i)
             if i == 6:
                 page_q.append(quantise_page(0, ["res6", "res7"]))
 
-        v2_plane = sb("v2_plane", [P, S], U8, tag="h1")
-        v2_codes = [sb("v2_codes0", [P, S], U32, tag="wg_last"), sb("v2_codes1", [P, S], U32, tag="h0")]
+        v2_plane = sb("v2_plane", [P, S], U8, tag="placed1")
+        v2_codes = [sb("v2_codes0", [P, S], U32, tag="placed0"), sb("v2_codes1", [P, S], U32, tag="wg_last")]
         nc.vector.tensor_copy(v2_plane[:], tab2_plane[:].indirect(idx2[:]))
         for a in range(2):
             nc.vector.tensor_copy(v2_codes[a][:], tab2_w[a][:].bitcast(U32).indirect(idx2[:]))

@@ -22,6 +22,11 @@ PASS = P * PACK
 BANK = 512
 QUAD = 32
 LIVE = 4
+SLICES = H // P
+HALF = S // 2
+QUAD_ORDER = (0, 2, 1, 3)
+W1_SPLIT = 80
+MID = 2304
 
 
 def tile_list_dredge_streak_scores_kernel(
@@ -31,10 +36,14 @@ def tile_list_dredge_streak_scores_kernel(
     nc = tc.nc
     with ExitStack() as ctx:
         keep = ctx.enter_context(tc.tile_pool(name="keep", bufs=1))
+        late = ctx.enter_context(tc.tile_pool(name="late", bufs=1))
         psum = ctx.enter_context(tc.psum_pool(name="psum", bufs=1))
 
         def sb(name, shape, dtype, tag=None, bufs=1):
             return keep.tile(shape, dtype, name=name, tag=tag or name, bufs=bufs, align_bytes=64)
+
+        def sb_at(name, shape, dtype, offset):
+            return late.tile(shape, dtype, name=name, tag=name, align_bytes=64, offset=offset)
 
         def bank(b, name, shape):
             return psum.tile(shape, F32, name=name, tag="bank%d" % b)
@@ -51,8 +60,15 @@ def tile_list_dredge_streak_scores_kernel(
         nc.vector.memset(w4_plane_raw[:].bitcast(I32), 0)
         nc.gpsimd.memset(tab2_plane[:].bitcast(I32), 0)
 
+        def load_planes(plane, src):
+            for q in QUAD_ORDER:
+                nc.sync.dma_start(
+                    plane[QUAD * q : QUAD * q + LIVE, :, :].bitcast(I32),
+                    src[:, LIVE * q : LIVE * (q + 1), :].rearrange("a r c -> r a c").bitcast(I32),
+                )
+
         def load_packed_plane(plane, src):
-            for q in range(4):
+            for q in QUAD_ORDER:
                 nc.sync.dma_start(
                     plane[QUAD * q : QUAD * q + 2 * LIVE, :].bitcast(I32), src[:, LIVE * q : LIVE * (q + 1), :].bitcast(I32)
                 )
@@ -62,63 +78,61 @@ def tile_list_dredge_streak_scores_kernel(
             nc.sync.dma_start(t[:], src.rearrange("p t i -> p (t i)").bitcast(I32))
             return t
 
-        def load_w1(name, a, cols):
-            t = sb(name, [P, PACK, cols.stop - cols.start], F32)
-            nc.sync.dma_start(t[:], w1[PASS * a : PASS * (a + 1), cols].rearrange("(p j) c -> p j c", j=PACK))
+        def load_weight(name, rows):
+            t = sb(name, [P, PACK, PASS], F32)
+            nc.sync.dma_start(t[:], rows)
             return t
 
-        w4_raw = sb("w4_raw", [P, 2, 2 * H], U8)
-        nc.sync.dma_start(w4_raw[:].bitcast(I32), w4_words.rearrange("a p c -> p a c").bitcast(I32))
-        idx = load_list("idx", offs)
-        gain_sb = sb("gain_sb", [P, PACK], F32)
-        nc.sync.dma_start(gain_sb[:], gain.rearrange("(p t) -> p t", t=PACK))
-        idx3 = load_list("idx3", offs3)
-        w1_raw0 = load_w1("w1_raw0", 0, slice(0, R))
-        load_packed_plane(tab_plane, tab_scales)
-        tab_w = [load_words("tab_w0", tab_words[0], T)]
-        for q in range(4):
-            nc.sync.dma_start(
-                w4_plane_raw[QUAD * q : QUAD * q + LIVE, :, :].bitcast(I32),
-                w4_scales[:, LIVE * q : LIVE * (q + 1), :].rearrange("a r c -> r a c").bitcast(I32),
-            )
-        tab_w.append(load_words("tab_w1", tab_words[1], T))
-        w1_raw1 = [load_w1("w1_raw1%d" % h, 1, slice(256 * h, 256 * (h + 1))) for h in range(2)]
-
-        w2_rows = w2.rearrange("(p j) c -> p j c", j=PACK)
-        wgs_rows = wgs.rearrange("(p t) j -> p t j", t=PACK)
+        w1_rows = w1.rearrange("(a p j) c -> a p j c", p=P, j=PACK)
+        w2_rows = w2.rearrange("(p j) (a c) -> a p j c", j=PACK, c=PASS)
+        wgs_rows = wgs.rearrange("(p u t) j -> u p t j", u=2, t=2)
         res_rows = res.rearrange("(a p t) j -> a t p j", p=P, t=PACK)
         page_rows = page0.rearrange("(a p t) c -> a t p c", p=P, t=PACK)
-        w2_raw = [sb("w2_raw%d" % a, [P, PACK, PASS], F32) for a in range(2)]
-        res_sb = [sb("res%d" % i, [P, S], F32) for i in range(8)]
-        page = [sb("page%d" % i, [P, T2], F32) for i in range(8)]
-        wg_first = sb("wg_first", [P, 1, S], F32)
-        wg_rest = sb("wg_last", [P, PACK - 1, S], F32)
-
-        def load_w2(a):
-            nc.sync.dma_start(w2_raw[a][:], w2_rows[:, :, PASS * a : PASS * (a + 1)])
+        res_sb = [sb("res%d" % i, [P, S], F32) for i in range(SLICES)]
+        page = [sb("page%d" % i, [P, T2], F32) for i in range(SLICES)]
+        wg = [sb("wg%d" % u, [P, 2, S], F32) for u in range(2)]
 
         def load_slice(i):
             a, t = divmod(i, PACK)
             nc.sync.dma_start(res_sb[i][:], res_rows[a, t])
+            if i in (0, 2):
+                for q in QUAD_ORDER:
+                    nc.sync.dma_start(wg[i // 2][QUAD * q : QUAD * (q + 1), :, :], wgs_rows[i // 2])
             nc.sync.dma_start(page[i][:], page_rows[a, t])
 
-        load_w2(0)
-        for q in range(4):
-            nc.sync.dma_start(wg_first[QUAD * q : QUAD * (q + 1), :, :], wgs_rows[:, 0:1, :])
+        w4_raw = sb("w4_raw", [P, 2, 2 * H], U8)
+        nc.sync.dma_start(w4_raw[:].bitcast(I32), w4_words.rearrange("a p c -> p a c").bitcast(I32))
+        idx = load_list("idx", offs)
+        tab_w = [load_words("tab_w0", tab_words[0], T)]
+        w1_raw = [load_weight("w1_raw0", w1_rows[0])]
+        gain_sb = sb("gain_sb", [P, PACK], F32)
+        nc.sync.dma_start(gain_sb[:], gain.rearrange("(p t) -> p t", t=PACK))
+        load_packed_plane(tab_plane, tab_scales)
+        w1_raw.append(load_weight("w1_raw1", w1_rows[1]))
+        tab_w.append(load_words("tab_w1", tab_words[1], T))
+        load_planes(w4_plane_raw, w4_scales)
+        w2_raw = [load_weight("w2_raw0", w2_rows[0])]
+        v_plane = sb("v_plane", [P, S], U8)
+        v_plane_moved = sb("v_plane_moved", [P, S], U8)
+        nc.vector.tensor_copy(v_plane[:], tab_plane[:].indirect(idx[:]))
+        for q in QUAD_ORDER:
+            nc.gpsimd.dma_start(
+                v_plane_moved[QUAD * q : QUAD * q + LIVE, :].bitcast(I32),
+                v_plane[QUAD * q + LIVE : QUAD * q + 2 * LIVE, :].bitcast(I32),
+            )
         load_slice(0)
-        for q in range(4):
-            nc.sync.dma_start(wg_rest[QUAD * q : QUAD * (q + 1), :, :], wgs_rows[:, 1:PACK, :])
+        idx3 = load_list("idx3", offs3)
         load_slice(1)
-        load_w2(1)
-        for i in range(2, 4):
+        w2_raw.append(load_weight("w2_raw1", w2_rows[1]))
+        for i in range(2, 5):
             load_slice(i)
         idx2 = load_list("idx2", offs2)
-        p1 = load_list("p1", pos1)
-        p2 = load_list("p2", pos2)
         tab2_w = [load_words("tab2_w%d" % a, tab2_words[a], T3) for a in range(2)]
         load_packed_plane(tab2_plane, tab2_scales)
-        for i in range(4, 8):
+        for i in range(5, SLICES):
             load_slice(i)
+        p1 = load_list("p1", pos1)
+        p2 = load_list("p2", pos2)
         cut_sb = sb("cut_sb", [P, S // P], F32)
         with nc.allow_non_contiguous_dma(reason="one value a partition"):
             nc.sync.dma_start(cut_sb[:], cutoff.rearrange("(m p) -> p m", p=P))
@@ -129,196 +143,271 @@ def tile_list_dredge_streak_scores_kernel(
             w4_codes[:].bitcast(U16).rearrange("p k (a t m) -> p (k a) t m", a=2, t=PACK),
             w4_raw[:].bitcast(U16).rearrange("p k (a m t) -> p (k a) t m", a=2, t=PACK),
         )
-        nc.vector.tensor_copy(
-            w4_plane[:].rearrange("p k (a t m) -> p (k a) t m", a=2, t=PACK),
-            w4_plane_raw[:].rearrange("p k (a m t) -> p (k a) t m", a=2, t=PACK),
-        )
 
-        def round_weight(copy, rounded, raw, first, lo, hi):
+        def round_weight(copy, rounded, raw, ms=slice(0, P), ts=slice(0, PACK)):
             copy(
-                rounded[:].rearrange("p (t m j) -> p m t j", t=PACK, j=PACK)[:, lo:hi],
-                raw[:].rearrange("p j (m t) -> p m t j", t=PACK)[:, lo - first : hi - first],
+                rounded[:].rearrange("p (t m j) -> p m t j", t=PACK, j=PACK)[:, ms, ts, :],
+                raw[:].rearrange("p j (m t) -> p m t j", t=PACK)[:, ms, ts, :],
             )
 
         def rounded_tile(name, tag):
             return sb(name, [P, PACK * PASS], BF16, tag=tag)
 
-        def quantise(name, rounded, tag=None):
-            codes = sb(name + "_codes", [P, PASS], U32, tag=tag)
-            plane = sb(name + "_plane", [P, PASS], U8)
-            nc.vector.quantize_mx(out=codes[:].bitcast(FP8X4), scales=plane[:], in_=rounded[:])
-            return codes, plane
+        def quantised_tiles(name, width, tag=None):
+            return sb(name + "_codes", [P, width], U32, tag=tag), sb(name + "_plane", [P, width], U8)
 
-        v_plane = sb("v_plane", [P, S], U8)
-        v_plane_moved = sb("v_plane_moved", [P, S], U8)
-        v_codes = [sb("v_codes%d" % a, [P, S], U32) for a in range(2)]
-        nc.vector.tensor_copy(v_plane[:], tab_plane[:].indirect(idx[:]))
-        for q in range(4):
-            nc.gpsimd.dma_start(
-                v_plane_moved[QUAD * q : QUAD * q + LIVE, :].bitcast(I32),
-                v_plane[QUAD * q + LIVE : QUAD * q + 2 * LIVE, :].bitcast(I32),
+        def quantise(dst, cols, rounded):
+            codes, plane = dst
+            nc.vector.quantize_mx(out=codes[:, cols].bitcast(FP8X4), scales=plane[:, cols], in_=rounded)
+
+        def mx(acc, lhs, lhs_plane, rhs, rhs_plane, start, stop, lhs_dtype=FP8X4):
+            nc.tensor.matmul_mx(
+                out=acc, lhsT=lhs.bitcast(lhs_dtype), lhsT_scale=lhs_plane, rhs=rhs.bitcast(FP8X4), rhs_scale=rhs_plane,
+                start=start, stop=stop,
             )
-        for a in range(2):
-            nc.vector.tensor_copy(v_codes[a][:], tab_w[a][:].bitcast(U32).indirect(idx[:]))
 
+        whole = slice(0, PASS)
+        halves = [slice(HALF * h, HALF * (h + 1)) for h in range(2)]
+        list_halves = [slice(HALF // 16 * h, HALF // 16 * (h + 1)) for h in range(2)]
+
+        v_codes = [sb("v_codes%d" % a, [P, S], U32) for a in range(2)]
         w1_bf = [rounded_tile("w1_bf%d" % a, "bf%d" % a) for a in range(2)]
-        round_weight(nc.scalar.copy, w1_bf[0], w1_raw0, 0, 0, P)
-        round_weight(nc.scalar.copy, w1_bf[1], w1_raw1[0], 0, 0, 64)
-        round_weight(nc.scalar.copy, w1_bf[1], w1_raw1[1], 64, 64, 88)
-        round_weight(nc.vector.tensor_copy, w1_bf[1], w1_raw1[1], 64, 88, P)
-        w1_q = [quantise("w1_%d" % a, w1_bf[a]) for a in range(2)]
+        w1_q = [quantised_tiles("w1_%d" % a, PASS) for a in range(2)]
+        round_weight(nc.scalar.copy, w1_bf[0], w1_raw[0])
+        nc.vector.tensor_copy(v_codes[0][:], tab_w[0][:].bitcast(U32).indirect(idx[:]))
+        quantise(w1_q[0], whole, w1_bf[0][:])
+        round_weight(nc.scalar.copy, w1_bf[1], w1_raw[1], ms=slice(0, W1_SPLIT))
+        round_weight(nc.vector.tensor_copy, w1_bf[1], w1_raw[1], ms=slice(W1_SPLIT, P))
+        quantise(w1_q[1], whole, w1_bf[1][:])
+        for h in range(2):
+            nc.vector.tensor_copy(v_codes[1][:, halves[h]], tab_w[1][:].bitcast(U32).indirect(idx[:, list_halves[h]]))
+
+        def deal_w4_plane(a):
+            cols = slice(PASS * a, PASS * (a + 1))
+            nc.vector.tensor_copy(
+                w4_plane[:, :, cols].rearrange("p k (t m) -> p k t m", t=PACK),
+                w4_plane_raw[:, :, cols].rearrange("p k (m t) -> p k t m", t=PACK),
+            )
+
+        deal_w4_plane(0)
 
         z = [bank(q, "z%d" % q, [P, PACK, P]) for q in range(4)]
-        for a in range(2):
+        d_banks = [bank(4 + i, "d%d" % i, [P, S]) for i in range(4)]
+
+        def z_pass(a):
             codes, plane = w1_q[a]
             for q in range(4):
+                cols = slice(P * q, P * (q + 1))
                 for t in range(PACK):
-                    nc.tensor.matmul_mx(
-                        out=z[q][:, t, :],
-                        lhsT=codes[:, P * t : P * (t + 1)].bitcast(FP8X4), lhsT_scale=plane[:, P * t : P * (t + 1)],
-                        rhs=v_codes[a][:, P * q : P * (q + 1)].bitcast(FP8X4), rhs_scale=v_plane[LIVE * a : P, P * q : P * (q + 1)],
-                        start=(a == 0 and t == 0), stop=(a == 1 and t == PACK - 1),
+                    mx(
+                        z[q][:, t, :], codes[:, P * t : P * (t + 1)], plane[:, P * t : P * (t + 1)],
+                        v_codes[a][:, cols], v_plane[LIVE * a : P, cols], a == 0 and t == 0, a == 1 and t == PACK - 1,
                     )
-        x_codes = sb("x_codes", [P, S], U32)
-        x_plane = sb("x_plane", [P, S], U8)
+
+        def d_pass(i, k):
+            mx(
+                d_banks[i][:], w4_codes[:, k, 2 * P * i : 2 * P * (i + 1)], w4_plane[:, k, P * i : P * (i + 1)],
+                v_codes[k][:], (v_plane, v_plane_moved)[k][:], k == 0, k == 1, FP4X4,
+            )
+
+        for a in range(2):
+            z_pass(a)
+        for i in range(4):
+            for k in range(2):
+                d_pass(i, k)
+
+        d_sb = [sb("d_sb%d" % i, [P, S], F32) for i in range(SLICES)]
+
+        def empty_d(i):
+            nc.scalar.copy(d_sb[i][:], d_banks[i][:])
+
+        x_q = quantised_tiles("x", S)
         x_bf = [sb("x_bf%d" % h, [P, 2, P, PACK], BF16) for h in range(2)]
+        w2_bf = [rounded_tile("w2_bf%d" % a, "bf%d" % (2 + a)) for a in range(2)]
+        w2_q = [quantised_tiles("w2_0", PASS)]
+
+        def quantise_x(h):
+            quantise(x_q, halves[h], x_bf[h][:].rearrange("p q n t -> p (q n t)"))
+
         for q in range(4):
             th = sb("th%d" % q, [P, P, PACK], F32)
             nc.scalar.activation(th[:], z[q][:].rearrange("p t n -> p n t"), ACT.Tanh)
             nc.vector.tensor_tensor(
                 x_bf[q // 2][:, q % 2, :, :], th[:], gain_sb[:].unsqueeze(1).to_broadcast([P, P, PACK]), ALU.mult
             )
-        w2_bf = [rounded_tile("w2_bf%d" % a, "bf%d" % (2 + a)) for a in range(2)]
-        round_weight(nc.scalar.copy, w2_bf[0], w2_raw[0], 0, 0, 80)
-        round_weight(nc.vector.tensor_copy, w2_bf[0], w2_raw[0], 0, 80, P)
+            if q == 2:
+                quantise_x(0)
+        empty_d(0)
+        round_weight(nc.vector.tensor_copy, w2_bf[0], w2_raw[0], ts=slice(0, 2))
+        round_weight(nc.scalar.copy, w2_bf[0], w2_raw[0], ts=slice(2, PACK))
+        quantise_x(1)
         for h in range(2):
-            nc.vector.quantize_mx(
-                out=x_codes[:, 256 * h : 256 * (h + 1)].bitcast(FP8X4), scales=x_plane[:, 256 * h : 256 * (h + 1)],
-                in_=x_bf[h][:].rearrange("p q n t -> p (q n t)"),
-            )
-        w2_q = [quantise("w2_0", w2_bf[0])]
-
-        page_bf = [[sb("page_bf%d%d" % (a, h), [P, BANK, PACK], BF16, tag="bf%d" % (2 * a + h)) for h in range(2)] for a in range(1)]
-        page_q = []
-
-        def other_product(i):
-            a, t = divmod(i, PACK)
-            cols = slice(PASS * a + P * t, PASS * a + P * (t + 1))
-            d = bank(i % 4, "d%d" % i, [P, S])
-            for k in range(2):
-                nc.tensor.matmul_mx(
-                    out=d[:],
-                    lhsT=w4_codes[:, k, 2 * cols.start : 2 * cols.stop].bitcast(FP4X4), lhsT_scale=w4_plane[:, k, cols],
-                    rhs=v_codes[k][:].bitcast(FP8X4), rhs_scale=(v_plane, v_plane_moved)[k][:],
-                    start=(k == 0), stop=(k == 1),
-                )
-            d_sb = sb("d_sb%d" % i, [P, S], F32)
-            nc.scalar.copy(d_sb[:], d[:])
-            return d_sb
-
-        d_all = [other_product(i) for i in range(8)]
-        round_weight(nc.scalar.copy, w2_bf[1], w2_raw[1], 0, 0, P)
+            quantise(w2_q[0], halves[h], w2_bf[0][:, PACK * HALF * h : PACK * HALF * (h + 1)])
+        deal_w4_plane(1)
 
         def product(i):
             a, t = divmod(i, PACK)
-            d_sb = d_all[i]
-            b = bank(4 + i % 4, "b%d" % i, [P, S])
+            b = bank(i % 4, "b%d" % i, [P, S])
             codes, plane = w2_q[a]
-            nc.tensor.matmul_mx(
-                out=b[:],
-                lhsT=codes[:, P * t : P * (t + 1)].bitcast(FP8X4), lhsT_scale=plane[:, P * t : P * (t + 1)],
-                rhs=x_codes[:].bitcast(FP8X4), rhs_scale=x_plane[:], start=True, stop=True,
-            )
-            bd = sb("bd%d" % i, [P, S], F32, tag="bd", bufs=3)
-            nc.vector.tensor_tensor(bd[:], b[:], d_sb[:], ALU.mult)
+            mx(b[:], codes[:, P * t : P * (t + 1)], plane[:, P * t : P * (t + 1)], x_q[0][:], x_q[1][:], True, True)
+            if i in (4, 5):
+                bd = sb_at("bd%d" % i, [P, S], F32, MID + 4 * S * (i - 4))
+            else:
+                bd = sb("bd%d" % i, [P, S], F32, tag="slot%d" % (i % 6))
+            nc.vector.tensor_tensor(bd[:], b[:], d_sb[i][:], ALU.mult)
             return bd
 
+        def parts_of(i):
+            return list(zip(halves, list_halves)) if i == 0 else [(whole, slice(0, S // 16))]
+
         def weigh(i, bd):
-            t = i % PACK
-            wg = wg_first[:, 0, :] if t == 0 else wg_rest[:, t - 1, :]
-            h_sb = sb("h%d" % i, [P, S], F32, tag="h", bufs=2)
-            nc.gpsimd.tensor_tensor(h_sb[:], bd[:], res_sb[i][:], ALU.add)
-            placed = sb("placed%d" % i, [P, S], F32, tag="placed%d" % (i % 2))
-            nc.gpsimd.tensor_tensor(placed[:], h_sb[:], wg, ALU.mult)
+            h_sb = sb("h%d" % i, [P, S], F32, tag="bf3" if i == 3 else "h%d" % (i % 2))
+            if i == SLICES - 1:
+                placed = sb_at("placed_last", [P, S], F32, 0)
+            elif i == 2:
+                placed = sb_at("placed_mid", [P, S], F32, MID + 2 * S)
+            else:
+                placed = sb("placed%d" % i, [P, S], F32, tag="slot%d" % (i + 4 if i < 2 else i - 3))
+            for cols, entries in parts_of(i):
+                nc.gpsimd.tensor_tensor(h_sb[:, cols], bd[:, cols], res_sb[i][:, cols], ALU.add)
+                nc.gpsimd.tensor_tensor(placed[:, cols], h_sb[:, cols], wg[i % PACK // 2][:, i % 2, cols], ALU.mult)
             return placed
 
-        def round_page(i):
-            a, t = divmod(i, PACK)
-            for h in range(2):
-                nc.scalar.copy(page_bf[a][h][:, :, t], page[i][:, BANK * h : BANK * (h + 1)])
+        def scatter(i, placed):
+            for cols, entries in parts_of(i):
+                nc.vector.tensor_copy(page[i][:].indirect(idx3[:, entries]), placed[:, cols])
 
-        def quantise_page(a, tags):
-            return [quantise("page_%d%d" % (a, h), page_bf[a][h][:].rearrange("p c t -> p (c t)"), tags[h]) for h in range(2)]
+        for i in range(1, 4):
+            empty_d(i)
+        bds = [product(i) for i in range(4)]
+        for i in range(4, SLICES):
+            d_banks.append(bank(i, "d%d" % i, [P, S]))
+            for k in range(2):
+                d_pass(i, k)
+            empty_d(i)
+        round_weight(nc.scalar.copy, w2_bf[1], w2_raw[1])
 
-        bd = product(0)
-        placed = weigh(1, product(1))
-        h_first = sb("h0", [P, S], F32)
-        nc.vector.tensor_tensor(h_first[:], bd[:], res_sb[0][:], ALU.add)
-        nc.vector.tensor_tensor(page[0][:].indirect(idx3[:]), h_first[:], wg_first[:, 0, :], ALU.mult)
-        round_page(0)
-        for i in range(1, 8):
-            now = placed
+        first_bf = sb("page_bf0", [P, T2, PACK], BF16, tag="w2_raw1")
+        for i in range(PACK):
+            scatter(i, weigh(i, bds[i]))
+            nc.scalar.copy(first_bf[:, :, i], page[i][:])
+            if i == 1:
+                w2_q.append(quantised_tiles("w2_1", PASS, "slot5"))
+                quantise(w2_q[1], whole, w2_bf[1][:])
             if i == 2:
-                w2_q.append(quantise("w2_1", w2_bf[1]))
-                page_bf.append([sb("page_bf1%d" % h, [P, BANK, PACK], BF16, tag="bf%d" % (2 + h)) for h in range(2)])
-            if i < 7:
-                placed = weigh(i + 1, product(i + 1))
-            nc.vector.tensor_copy(page[i][:].indirect(idx3[:]), now[:])
-            round_page(i)
-            if i == 6:
-                page_q.append(quantise_page(0, ["res6", "res7"]))
+                bds.append(product(4))
+            if i >= 2:
+                bds.append(product(i + 3))
+        last_bf = [sb("page_bf1%d" % h, [P, BANK, PACK], BF16, tag="bf%d" % (2 + h)) for h in range(2)]
+        placed = weigh(PACK, bds[PACK])
+        for i in range(PACK, SLICES):
+            now = placed
+            if i + 1 < SLICES:
+                placed = weigh(i + 1, bds[i + 1])
+            else:
+                first_q = quantised_tiles("page_0", T2, "res7")
+                quantise(first_q, slice(0, T2), first_bf[:].rearrange("p c t -> p (c t)"))
+            scatter(i, now)
+            for h in range(2):
+                rounded, cols = last_bf[h][:, :, i - PACK], page[i][:, BANK * h : BANK * (h + 1)]
+                if h == 1 and i >= SLICES - 2:
+                    nc.gpsimd.tensor_scalar(rounded, cols, 1.0, 0.0, ALU.mult, ALU.add)
+                else:
+                    nc.scalar.copy(rounded, cols)
+            if i + 3 < SLICES:
+                bds.append(product(i + 3))
 
-        v2_plane = sb("v2_plane", [P, S], U8, tag="placed1")
-        v2_codes = [sb("v2_codes0", [P, S], U32, tag="placed0"), sb("v2_codes1", [P, S], U32, tag="wg_last")]
-        nc.vector.tensor_copy(v2_plane[:], tab2_plane[:].indirect(idx2[:]))
+        last_q = [quantised_tiles("page_1%d" % h, BANK) for h in range(2)]
+
+        def quantise_last(h):
+            quantise(last_q[h], whole, last_bf[h][:].rearrange("p c t -> p (c t)"))
+
+        def gather_v2_plane(plane, h):
+            nc.vector.tensor_copy(plane[:], tab2_plane[:].indirect(idx2[:, list_halves[h]]))
+
+        def gather_v2_codes(codes, a, first, count):
+            nc.vector.tensor_copy(codes, tab2_w[a][:].bitcast(U32).indirect(idx2[:, first // 16 : (first + count) // 16]))
+
+        v2_plane = [sb_at("v2_plane0", [P, HALF], U8, 0)]
+        gather_v2_plane(v2_plane[0], 0)
+        v2_codes = []
+        for m in range(2):
+            v2_codes.append([sb_at("v2_codes%d%d" % (m, a), [P, P], U32, HALF + 4 * P * (2 * m + a))[:] for a in range(2)])
+            for a in range(2):
+                gather_v2_codes(v2_codes[m][a], a, P * m, P)
+        quantise_last(0)
+        quantise_last(1)
+        v2_plane.append(sb("v2_plane1", [P, HALF], U8, tag="bf2"))
+        gather_v2_plane(v2_plane[1], 1)
+        v2_last = sb("v2_last", [P, 2, HALF], U32, tag="bf3")
         for a in range(2):
-            nc.vector.tensor_copy(v2_codes[a][:], tab2_w[a][:].bitcast(U32).indirect(idx2[:]))
-        page_q.append(quantise_page(1, [None, None]))
+            gather_v2_codes(v2_last[:, a, :], a, HALF, HALF)
+        for m in range(2):
+            v2_codes.append([v2_last[:, a, P * m : P * (m + 1)] for a in range(2)])
 
-        e_tags = ["tab_w0", "tab_w1", "w1_raw0", "w1_raw10"]
-
-        e_banks = [[None, None] for m in range(4)]
+        e_tags = ["tab_w0", "tab_w1", "w1_raw0", "w1_raw1"]
+        e_sb = [sb("e%d" % m, [P, T2], F32, tag=e_tags[m]) for m in range(4)]
+        e_banks = [[bank((4 + 2 * m + h) % 8, "e%d%d" % (m, h), [P, BANK]) for h in range(2)] for m in range(4)]
 
         def score_pass(m, h, a):
-            codes, plane = page_q[a][h]
-            nc.tensor.matmul_mx(
-                out=e_banks[m][h][:],
-                lhsT=v2_codes[a][:, P * m : P * (m + 1)].bitcast(FP8X4),
-                lhsT_scale=v2_plane[LIVE * a : P, P * m : P * (m + 1)],
-                rhs=codes[:].bitcast(FP8X4), rhs_scale=plane[:], start=(a == 0), stop=(a == 1),
+            cols = slice(P * (m % 2), P * (m % 2 + 1))
+            page_cols = slice(BANK * h, BANK * (h + 1)) if a == 0 else whole
+            codes, plane = first_q if a == 0 else last_q[h]
+            mx(
+                e_banks[m][h][:], v2_codes[m][a], v2_plane[m // 2][LIVE * a : P, cols],
+                codes[:, page_cols], plane[:, page_cols], a == 0, a == 1,
             )
 
-        e_all = []
-        for pair in range(2):
-            for m in (2 * pair, 2 * pair + 1):
+        for m in range(4):
+            for a in range(2):
                 for h in range(2):
-                    e_banks[m][h] = bank(2 * (m % 2) + h, "e%d%d" % (m, h), [P, BANK])
-                    score_pass(m, h, 0)
-            for m in (2 * pair, 2 * pair + 1):
-                e_sb = sb("e%d" % m, [P, T2], F32, tag=e_tags[m])
-                for h in range(2):
-                    score_pass(m, h, 1)
-                    nc.scalar.copy(e_sb[:, BANK * h : BANK * (h + 1)], e_banks[m][h][:])
-                e_all.append(e_sb)
+                    score_pass(m, h, a)
 
-        def pick_second(m, e_sb):
-            second = sb("second%d" % m, [P, S], F32, tag="second", bufs=2)
-            nc.vector.tensor_copy(second[:], e_sb[:].indirect(p2[:]))
-            return second
+        def empty_e(m):
+            for h in range(2):
+                nc.scalar.copy(e_sb[m][:, BANK * h : BANK * (h + 1)], e_banks[m][h][:])
 
-        def floor_second(m, second):
-            later = sb("later%d" % m, [P, S], F32, tag="later", bufs=2)
-            nc.vector.tensor_scalar_max(later[:], second[:], cut_sb[:, m : m + 1])
-            return later
+        minus_cut = sb("minus_cut", [P, S // P], F32)
+        nc.gpsimd.tensor_scalar(minus_cut[:], cut_sb[:], -1.0, 0.0, ALU.mult, ALU.add)
 
-        def finish(m, e_sb, later):
-            result = sb("result%d" % m, [P, S], F32, tag="result", bufs=3)
-            nc.vector.tensor_tensor(result[:], e_sb[:].indirect(p1[:]), later[:], ALU.subtract)
+        def pick(name, m, entries, tag):
+            picked = sb("%s%d" % (name, m), [P, S], F32, tag=tag)
+            nc.vector.tensor_copy(picked[:], e_sb[m][:].indirect(entries[:]))
+            return picked
+
+        def excess_over_cutoff(m, second):
+            excess = sb("excess%d" % m, [P, S], F32, tag="th%d" % m)
+            nc.scalar.activation(excess[:], second[:], ACT.Relu, bias=minus_cut[:, m : m + 1])
+            return excess
+
+        def finish_plain(m, first, excess):
+            gap = sb("gap%d" % m, [P, S], F32, tag="res%d" % m)
+            nc.gpsimd.tensor_tensor(gap[:], first[:], excess[:], ALU.subtract)
+            result = sb("result%d" % m, [P, S], F32, tag="slot%d" % m)
+            nc.gpsimd.tensor_scalar(result[:], gap[:], 1.0, minus_cut[:, m : m + 1], ALU.mult, ALU.add)
             nc.sync.dma_start(out[P * m : P * (m + 1), :], result[:])
 
-        later = floor_second(0, pick_second(0, e_all[0]))
-        for m in range(1, 4):
-            second = pick_second(m, e_all[m])
-            finish(m - 1, e_all[m - 1], later)
-            later = floor_second(m, second)
-        finish(3, e_all[3], later)
+        def later_score(m, second):
+            later = sb("later%d" % m, [P, S], F32, tag="res%d" % m)
+            nc.scalar.activation(later[:], excess_over_cutoff(m, second)[:], ACT.Identity, bias=cut_sb[:, m : m + 1])
+            return later
+
+        def finish_fused(m, later, parts):
+            result = sb("result%d" % m, [P, S], F32, tag="slot%d" % m)
+            for cols, entries in parts:
+                nc.vector.tensor_tensor(result[:, cols], e_sb[m][:].indirect(p1[:, entries]), later[:, cols], ALU.subtract)
+                nc.sync.dma_start(out[P * m : P * (m + 1), cols], result[:, cols])
+
+        empty_e(0)
+        empty_e(1)
+        for m in range(2):
+            second = pick("second", m, p2, "d_sb%d" % m)
+            first = pick("first", m, p1, "d_sb%d" % (4 + m))
+            excess = excess_over_cutoff(m, second)
+            if m == 0:
+                empty_e(2)
+                empty_e(3)
+            finish_plain(m, first, excess)
+        laters = [later_score(m, pick("second", m, p2, "d_sb%d" % m)) for m in (2, 3)]
+        finish_fused(2, laters[0], [(whole, slice(0, S // 16))])
+        finish_fused(3, laters[1], list(zip(halves, list_halves)))

@@ -26,7 +26,7 @@ SLICES = H // P
 HALF = S // 2
 QUAD_ORDER = (0, 2, 1, 3)
 W1_SPLIT = 80
-MID = 2304
+MID = 2048
 
 
 def tile_list_dredge_streak_scores_kernel(
@@ -309,11 +309,7 @@ def tile_list_dredge_streak_scores_kernel(
                 quantise(first_q, slice(0, T2), first_bf[:].rearrange("p c t -> p (c t)"))
             scatter(i, now)
             for h in range(2):
-                rounded, cols = last_bf[h][:, :, i - PACK], page[i][:, BANK * h : BANK * (h + 1)]
-                if h == 1 and i >= SLICES - 2:
-                    nc.gpsimd.tensor_scalar(rounded, cols, 1.0, 0.0, ALU.mult, ALU.add)
-                else:
-                    nc.scalar.copy(rounded, cols)
+                nc.scalar.copy(last_bf[h][:, :, i - PACK], page[i][:, BANK * h : BANK * (h + 1)])
             if i + 3 < SLICES:
                 bds.append(product(i + 3))
 
@@ -328,17 +324,18 @@ def tile_list_dredge_streak_scores_kernel(
         def gather_v2_codes(codes, a, first, count):
             nc.vector.tensor_copy(codes, tab2_w[a][:].bitcast(U32).indirect(idx2[:, first // 16 : (first + count) // 16]))
 
-        v2_plane = [sb_at("v2_plane0", [P, HALF], U8, 0)]
+        v2_plane = [sb_at("v2_plane%d" % h, [P, HALF], U8, HALF * h) for h in range(2)]
+        v2_codes = [[sb_at("v2_codes0%d" % a, [P, P], U32, S + 4 * P * a)[:] for a in range(2)]]
         gather_v2_plane(v2_plane[0], 0)
-        v2_codes = []
-        for m in range(2):
-            v2_codes.append([sb_at("v2_codes%d%d" % (m, a), [P, P], U32, HALF + 4 * P * (2 * m + a))[:] for a in range(2)])
-            for a in range(2):
-                gather_v2_codes(v2_codes[m][a], a, P * m, P)
-        quantise_last(0)
-        quantise_last(1)
-        v2_plane.append(sb("v2_plane1", [P, HALF], U8, tag="bf2"))
+        for a in range(2):
+            gather_v2_codes(v2_codes[0][a], a, 0, P)
         gather_v2_plane(v2_plane[1], 1)
+        quantise_last(0)
+        v2_second = sb("v2_second", [P, 2, P], U32, tag="bf2")
+        v2_codes.append([v2_second[:, a, :] for a in range(2)])
+        for a in range(2):
+            gather_v2_codes(v2_codes[1][a], a, P, P)
+        quantise_last(1)
         v2_last = sb("v2_last", [P, 2, HALF], U32, tag="bf3")
         for a in range(2):
             gather_v2_codes(v2_last[:, a, :], a, HALF, HALF)

from contextlib import ExitStack

import concourse.mybir as mybir

K, R, H, T, S, T3, T2 = 1024, 512, 1024, 2048, 512, 1024, 1024
FLOPS = 2 * (K * R * S + R * H * S + K * H * S + H * S * T2)

F32 = mybir.dt.float32
BF16 = mybir.dt.bfloat16
I32 = mybir.dt.int32
U32 = mybir.dt.uint32
U16 = mybir.dt.uint16
U8 = mybir.dt.uint8
FP8X4 = mybir.dt.float8_e4m3fn_x4
FP4X4 = mybir.dt.float4_e2m1fn_x4
ALU = mybir.AluOpType
ACT = mybir.ActivationFunctionType

P = 128
PACK = 4
PASS = P * PACK
BANK = 512
QUAD = 32
LIVE = 4
SLICES = H // P
HALF = S // 2
QUAD_ORDER = (0, 2, 1, 3)
W1_SPLIT = 80
MID = 2048


def tile_list_dredge_streak_scores_kernel(
    tc, tab_words, tab_scales, tab2_words, tab2_scales, w4_words, w4_scales, w1, gain, w2, res, wgs, page0, cutoff,
    offs, offs2, offs3, pos1, pos2, out,
):
    nc = tc.nc
    with ExitStack() as ctx:
        keep = ctx.enter_context(tc.tile_pool(name="keep", bufs=1))
        late = ctx.enter_context(tc.tile_pool(name="late", bufs=1))
        psum = ctx.enter_context(tc.psum_pool(name="psum", bufs=1))

        def sb(name, shape, dtype, tag=None, bufs=1):
            return keep.tile(shape, dtype, name=name, tag=tag or name, bufs=bufs, align_bytes=64)

        def sb_at(name, shape, dtype, offset):
            return late.tile(shape, dtype, name=name, tag=name, align_bytes=64, offset=offset)

        def bank(b, name, shape):
            return psum.tile(shape, F32, name=name, tag="bank%d" % b)

        def load_list(name, src):
            t = keep.tile([P, S // 16], U16, name=name)
            nc.sync.dma_start(t[:], src)
            return t

        tab_plane = sb("tab_plane", [P, T], U8)
        w4_plane_raw = sb("w4_plane_raw", [P, 2, H], U8)
        tab2_plane = sb("tab2_plane", [P, T3], U8)
        nc.gpsimd.memset(tab_plane[:].bitcast(I32), 0)
        nc.vector.memset(w4_plane_raw[:].bitcast(I32), 0)
        nc.gpsimd.memset(tab2_plane[:].bitcast(I32), 0)

        def load_planes(plane, src):
            for q in QUAD_ORDER:
                nc.sync.dma_start(
                    plane[QUAD * q : QUAD * q + LIVE, :, :].bitcast(I32),
                    src[:, LIVE * q : LIVE * (q + 1), :].rearrange("a r c -> r a c").bitcast(I32),
                )

        def load_packed_plane(plane, src):
            for q in QUAD_ORDER:
                nc.sync.dma_start(
                    plane[QUAD * q : QUAD * q + 2 * LIVE, :].bitcast(I32), src[:, LIVE * q : LIVE * (q + 1), :].bitcast(I32)
                )

        def load_words(name, src, width):
            t = sb(name, [P, width], I32)
            nc.sync.dma_start(t[:], src.rearrange("p t i -> p (t i)").bitcast(I32))
            return t

        def load_weight(name, rows):
            t = sb(name, [P, PACK, PASS], F32)
            nc.sync.dma_start(t[:], rows)
            return t

        w1_rows = w1.rearrange("(a p j) c -> a p j c", p=P, j=PACK)
        w2_rows = w2.rearrange("(p j) (a c) -> a p j c", j=PACK, c=PASS)
        wgs_rows = wgs.rearrange("(p u t) j -> u p t j", u=2, t=2)
        res_rows = res.rearrange("(a p t) j -> a t p j", p=P, t=PACK)
        page_rows = page0.rearrange("(a p t) c -> a t p c", p=P, t=PACK)
        res_sb = [sb("res%d" % i, [P, S], F32) for i in range(SLICES)]
        page = [sb("page%d" % i, [P, T2], F32) for i in range(SLICES)]
        wg = [sb("wg%d" % u, [P, 2, S], F32) for u in range(2)]

        def load_slice(i):
            a, t = divmod(i, PACK)
            nc.sync.dma_start(res_sb[i][:], res_rows[a, t])
            if i in (0, 2):
                for q in QUAD_ORDER:
                    nc.sync.dma_start(wg[i // 2][QUAD * q : QUAD * (q + 1), :, :], wgs_rows[i // 2])
            nc.sync.dma_start(page[i][:], page_rows[a, t])

        w4_raw = sb("w4_raw", [P, 2, 2 * H], U8)
        nc.sync.dma_start(w4_raw[:].bitcast(I32), w4_words.rearrange("a p c -> p a c").bitcast(I32))
        idx = load_list("idx", offs)
        tab_w = [load_words("tab_w0", tab_words[0], T)]
        w1_raw = [load_weight("w1_raw0", w1_rows[0])]
        gain_sb = sb("gain_sb", [P, PACK], F32)
        nc.sync.dma_start(gain_sb[:], gain.rearrange("(p t) -> p t", t=PACK))
        load_packed_plane(tab_plane, tab_scales)
        w1_raw.append(load_weight("w1_raw1", w1_rows[1]))
        tab_w.append(load_words("tab_w1", tab_words[1], T))
        load_planes(w4_plane_raw, w4_scales)
        w2_raw = [load_weight("w2_raw0", w2_rows[0])]
        v_plane = sb("v_plane", [P, S], U8)
        v_plane_moved = sb("v_plane_moved", [P, S], U8)
        nc.vector.tensor_copy(v_plane[:], tab_plane[:].indirect(idx[:]))
        for q in QUAD_ORDER:
            nc.gpsimd.dma_start(
                v_plane_moved[QUAD * q : QUAD * q + LIVE, :].bitcast(I32),
                v_plane[QUAD * q + LIVE : QUAD * q + 2 * LIVE, :].bitcast(I32),
            )
        load_slice(0)
        idx3 = load_list("idx3", offs3)
        load_slice(1)
        w2_raw.append(load_weight("w2_raw1", w2_rows[1]))
        for i in range(2, 5):
            load_slice(i)
        idx2 = load_list("idx2", offs2)
        tab2_w = [load_words("tab2_w%d" % a, tab2_words[a], T3) for a in range(2)]
        load_packed_plane(tab2_plane, tab2_scales)
        for i in range(5, SLICES):
            load_slice(i)
        p1 = load_list("p1", pos1)
        p2 = load_list("p2", pos2)
        cut_sb = sb("cut_sb", [P, S // P], F32)
        with nc.allow_non_contiguous_dma(reason="one value a partition"):
            nc.sync.dma_start(cut_sb[:], cutoff.rearrange("(m p) -> p m", p=P))

        w4_codes = sb("w4_codes", [P, 2, 2 * H], U8)
        w4_plane = sb("w4_plane", [P, 2, H], U8)
        nc.vector.tensor_copy(
            w4_codes[:].bitcast(U16).rearrange("p k (a t m) -> p (k a) t m", a=2, t=PACK),
            w4_raw[:].bitcast(U16).rearrange("p k (a m t) -> p (k a) t m", a=2, t=PACK),
        )

        def round_weight(copy, rounded, raw, ms=slice(0, P), ts=slice(0, PACK)):
            copy(
                rounded[:].rearrange("p (t m j) -> p m t j", t=PACK, j=PACK)[:, ms, ts, :],
                raw[:].rearrange("p j (m t) -> p m t j", t=PACK)[:, ms, ts, :],
            )

        def rounded_tile(name, tag):
            return sb(name, [P, PACK * PASS], BF16, tag=tag)

        def quantised_tiles(name, width, tag=None):
            return sb(name + "_codes", [P, width], U32, tag=tag), sb(name + "_plane", [P, width], U8)

        def quantise(dst, cols, rounded):
            codes, plane = dst
            nc.vector.quantize_mx(out=codes[:, cols].bitcast(FP8X4), scales=plane[:, cols], in_=rounded)

        def mx(acc, lhs, lhs_plane, rhs, rhs_plane, start, stop, lhs_dtype=FP8X4):
            nc.tensor.matmul_mx(
                out=acc, lhsT=lhs.bitcast(lhs_dtype), lhsT_scale=lhs_plane, rhs=rhs.bitcast(FP8X4), rhs_scale=rhs_plane,
                start=start, stop=stop,
            )

        whole = slice(0, PASS)
        halves = [slice(HALF * h, HALF * (h + 1)) for h in range(2)]
        list_halves = [slice(HALF // 16 * h, HALF // 16 * (h + 1)) for h in range(2)]

        v_codes = [sb("v_codes%d" % a, [P, S], U32) for a in range(2)]
        w1_bf = [rounded_tile("w1_bf%d" % a, "bf%d" % a) for a in range(2)]
        w1_q = [quantised_tiles("w1_%d" % a, PASS) for a in range(2)]
        round_weight(nc.scalar.copy, w1_bf[0], w1_raw[0])
        nc.vector.tensor_copy(v_codes[0][:], tab_w[0][:].bitcast(U32).indirect(idx[:]))
        quantise(w1_q[0], whole, w1_bf[0][:])
        round_weight(nc.scalar.copy, w1_bf[1], w1_raw[1], ms=slice(0, W1_SPLIT))
        round_weight(nc.vector.tensor_copy, w1_bf[1], w1_raw[1], ms=slice(W1_SPLIT, P))
        quantise(w1_q[1], whole, w1_bf[1][:])
        for h in range(2):
            nc.vector.tensor_copy(v_codes[1][:, halves[h]], tab_w[1][:].bitcast(U32).indirect(idx[:, list_halves[h]]))

        def deal_w4_plane(a):
            cols = slice(PASS * a, PASS * (a + 1))
            nc.vector.tensor_copy(
                w4_plane[:, :, cols].rearrange("p k (t m) -> p k t m", t=PACK),
                w4_plane_raw[:, :, cols].rearrange("p k (m t) -> p k t m", t=PACK),
            )

        deal_w4_plane(0)

        z = [bank(q, "z%d" % q, [P, PACK, P]) for q in range(4)]
        d_banks = [bank(4 + i, "d%d" % i, [P, S]) for i in range(4)]

        def z_pass(a):
            codes, plane = w1_q[a]
            for q in range(4):
                cols = slice(P * q, P * (q + 1))
                for t in range(PACK):
                    mx(
                        z[q][:, t, :], codes[:, P * t : P * (t + 1)], plane[:, P * t : P * (t + 1)],
                        v_codes[a][:, cols], v_plane[LIVE * a : P, cols], a == 0 and t == 0, a == 1 and t == PACK - 1,
                    )

        def d_pass(i, k):
            mx(
                d_banks[i][:], w4_codes[:, k, 2 * P * i : 2 * P * (i + 1)], w4_plane[:, k, P * i : P * (i + 1)],
                v_codes[k][:], (v_plane, v_plane_moved)[k][:], k == 0, k == 1, FP4X4,
            )

        for a in range(2):
            z_pass(a)
        for i in range(4):
            for k in range(2):
                d_pass(i, k)

        d_sb = [sb("d_sb%d" % i, [P, S], F32) for i in range(SLICES)]

        def empty_d(i):
            nc.scalar.copy(d_sb[i][:], d_banks[i][:])

        x_q = quantised_tiles("x", S)
        x_bf = [sb("x_bf%d" % h, [P, 2, P, PACK], BF16) for h in range(2)]
        w2_bf = [rounded_tile("w2_bf%d" % a, "bf%d" % (2 + a)) for a in range(2)]
        w2_q = [quantised_tiles("w2_0", PASS)]

        def quantise_x(h):
            quantise(x_q, halves[h], x_bf[h][:].rearrange("p q n t -> p (q n t)"))

        for q in range(4):
            th = sb("th%d" % q, [P, P, PACK], F32)
            nc.scalar.activation(th[:], z[q][:].rearrange("p t n -> p n t"), ACT.Tanh)
            nc.vector.tensor_tensor(
                x_bf[q // 2][:, q % 2, :, :], th[:], gain_sb[:].unsqueeze(1).to_broadcast([P, P, PACK]), ALU.mult
            )
            if q == 2:
                quantise_x(0)
        empty_d(0)
        round_weight(nc.vector.tensor_copy, w2_bf[0], w2_raw[0], ts=slice(0, 2))
        round_weight(nc.scalar.copy, w2_bf[0], w2_raw[0], ts=slice(2, PACK))
        quantise_x(1)
        for h in range(2):
            quantise(w2_q[0], halves[h], w2_bf[0][:, PACK * HALF * h : PACK * HALF * (h + 1)])
        deal_w4_plane(1)

        def product(i):
            a, t = divmod(i, PACK)
            b = bank(i % 4, "b%d" % i, [P, S])
            codes, plane = w2_q[a]
            mx(b[:], codes[:, P * t : P * (t + 1)], plane[:, P * t : P * (t + 1)], x_q[0][:], x_q[1][:], True, True)
            if i in (4, 5):
                bd = sb_at("bd%d" % i, [P, S], F32, MID + 4 * S * (i - 4))
            else:
                bd = sb("bd%d" % i, [P, S], F32, tag="slot%d" % (i % 6))
            nc.vector.tensor_tensor(bd[:], b[:], d_sb[i][:], ALU.mult)
            return bd

        def parts_of(i):
            return list(zip(halves, list_halves)) if i == 0 else [(whole, slice(0, S // 16))]

        def weigh(i, bd):
            h_sb = sb("h%d" % i, [P, S], F32, tag="bf3" if i == 3 else "h%d" % (i % 2))
            if i == SLICES - 1:
                placed = sb_at("placed_last", [P, S], F32, 0)
            elif i == 2:
                placed = sb_at("placed_mid", [P, S], F32, MID + 2 * S)
            else:
                placed = sb("placed%d" % i, [P, S], F32, tag="slot%d" % (i + 4 if i < 2 else i - 3))
            for cols, entries in parts_of(i):
                nc.gpsimd.tensor_tensor(h_sb[:, cols], bd[:, cols], res_sb[i][:, cols], ALU.add)
                nc.gpsimd.tensor_tensor(placed[:, cols], h_sb[:, cols], wg[i % PACK // 2][:, i % 2, cols], ALU.mult)
            return placed

        def scatter(i, placed):
            for cols, entries in parts_of(i):
                nc.vector.tensor_copy(page[i][:].indirect(idx3[:, entries]), placed[:, cols])

        for i in range(1, 4):
            empty_d(i)
        bds = [product(i) for i in range(4)]
        for i in range(4, SLICES):
            d_banks.append(bank(i, "d%d" % i, [P, S]))
            for k in range(2):
                d_pass(i, k)
            empty_d(i)
        round_weight(nc.scalar.copy, w2_bf[1], w2_raw[1])

        first_bf = sb("page_bf0", [P, T2, PACK], BF16, tag="w2_raw1")
        for i in range(PACK):
            scatter(i, weigh(i, bds[i]))
            nc.scalar.copy(first_bf[:, :, i], page[i][:])
            if i == 1:
                w2_q.append(quantised_tiles("w2_1", PASS, "slot5"))
                quantise(w2_q[1], whole, w2_bf[1][:])
            if i == 2:
                bds.append(product(4))
            if i >= 2:
                bds.append(product(i + 3))
        last_bf = [sb("page_bf1%d" % h, [P, BANK, PACK], BF16, tag="bf%d" % (2 + h)) for h in range(2)]
        placed = weigh(PACK, bds[PACK])
        for i in range(PACK, SLICES):
            now = placed
            if i + 1 < SLICES:
                placed = weigh(i + 1, bds[i + 1])
            else:
                first_q = quantised_tiles("page_0", T2, "res7")
                quantise(first_q, slice(0, T2), first_bf[:].rearrange("p c t -> p (c t)"))
            scatter(i, now)
            for h in range(2):
                nc.scalar.copy(last_bf[h][:, :, i - PACK], page[i][:, BANK * h : BANK * (h + 1)])
            if i + 3 < SLICES:
                bds.append(product(i + 3))

        last_q = [quantised_tiles("page_1%d" % h, BANK) for h in range(2)]

        def quantise_last(h):
            quantise(last_q[h], whole, last_bf[h][:].rearrange("p c t -> p (c t)"))

        def gather_v2_plane(plane, h):
            nc.vector.tensor_copy(plane[:], tab2_plane[:].indirect(idx2[:, list_halves[h]]))

        def gather_v2_codes(codes, a, first, count):
            nc.vector.tensor_copy(codes, tab2_w[a][:].bitcast(U32).indirect(idx2[:, first // 16 : (first + count) // 16]))

        v2_plane = [sb_at("v2_plane%d" % h, [P, HALF], U8, HALF * h) for h in range(2)]
        v2_codes = [[sb_at("v2_codes0%d" % a, [P, P], U32, S + 4 * P * a)[:] for a in range(2)]]
        gather_v2_plane(v2_plane[0], 0)
        for a in range(2):
            gather_v2_codes(v2_codes[0][a], a, 0, P)
        gather_v2_plane(v2_plane[1], 1)
        quantise_last(0)
        v2_second = sb("v2_second", [P, 2, P], U32, tag="bf2")
        v2_codes.append([v2_second[:, a, :] for a in range(2)])
        for a in range(2):
            gather_v2_codes(v2_codes[1][a], a, P, P)
        quantise_last(1)
        v2_last = sb("v2_last", [P, 2, HALF], U32, tag="bf3")
        for a in range(2):
            gather_v2_codes(v2_last[:, a, :], a, HALF, HALF)
        for m in range(2):
            v2_codes.append([v2_last[:, a, P * m : P * (m + 1)] for a in range(2)])

        e_tags = ["tab_w0", "tab_w1", "w1_raw0", "w1_raw1"]
        e_sb = [sb("e%d" % m, [P, T2], F32, tag=e_tags[m]) for m in range(4)]
        e_banks = [[bank((4 + 2 * m + h) % 8, "e%d%d" % (m, h), [P, BANK]) for h in range(2)] for m in range(4)]

        def score_pass(m, h, a):
            cols = slice(P * (m % 2), P * (m % 2 + 1))
            page_cols = slice(BANK * h, BANK * (h + 1)) if a == 0 else whole
            codes, plane = first_q if a == 0 else last_q[h]
            mx(
                e_banks[m][h][:], v2_codes[m][a], v2_plane[m // 2][LIVE * a : P, cols],
                codes[:, page_cols], plane[:, page_cols], a == 0, a == 1,
            )

        for m in range(4):
            for a in range(2):
                for h in range(2):
                    score_pass(m, h, a)

        def empty_e(m):
            for h in range(2):
                nc.scalar.copy(e_sb[m][:, BANK * h : BANK * (h + 1)], e_banks[m][h][:])

        minus_cut = sb("minus_cut", [P, S // P], F32)
        nc.gpsimd.tensor_scalar(minus_cut[:], cut_sb[:], -1.0, 0.0, ALU.mult, ALU.add)

        def pick(name, m, entries, tag):
            picked = sb("%s%d" % (name, m), [P, S], F32, tag=tag)
            nc.vector.tensor_copy(picked[:], e_sb[m][:].indirect(entries[:]))
            return picked

        def excess_over_cutoff(m, second):
            excess = sb("excess%d" % m, [P, S], F32, tag="th%d" % m)
            nc.scalar.activation(excess[:], second[:], ACT.Relu, bias=minus_cut[:, m : m + 1])
            return excess

        def finish_plain(m, first, excess):
            gap = sb("gap%d" % m, [P, S], F32, tag="res%d" % m)
            nc.gpsimd.tensor_tensor(gap[:], first[:], excess[:], ALU.subtract)
            result = sb("result%d" % m, [P, S], F32, tag="slot%d" % m)
            nc.gpsimd.tensor_scalar(result[:], gap[:], 1.0, minus_cut[:, m : m + 1], ALU.mult, ALU.add)
            nc.sync.dma_start(out[P * m : P * (m + 1), :], result[:])

        def later_score(m, second):
            later = sb("later%d" % m, [P, S], F32, tag="res%d" % m)
            nc.scalar.activation(later[:], excess_over_cutoff(m, second)[:], ACT.Identity, bias=cut_sb[:, m : m + 1])
            return later

        def finish_fused(m, later, parts):
            result = sb("result%d" % m, [P, S], F32, tag="slot%d" % m)
            for cols, entries in parts:
                nc.vector.tensor_tensor(result[:, cols], e_sb[m][:].indirect(p1[:, entries]), later[:, cols], ALU.subtract)
                nc.sync.dma_start(out[P * m : P * (m + 1), cols], result[:, cols])

        empty_e(0)
        empty_e(1)
        for m in range(2):
            second = pick("second", m, p2, "d_sb%d" % m)
            first = pick("first", m, p1, "d_sb%d" % (4 + m))
            excess = excess_over_cutoff(m, second)
            if m == 0:
                empty_e(2)
                empty_e(3)
            finish_plain(m, first, excess)
        laters = [later_score(m, pick("second", m, p2, "d_sb%d" % m)) for m in (2, 3)]
        finish_fused(2, laters[0], [(whole, slice(0, S // 16))])
        finish_fused(3, laters[1], list(zip(halves, list_halves)))
